import numpy as np
import ml_dtypes


def mxq(x, axis, fmt="e4m3"):
    dtype, down = {"e4m3": (ml_dtypes.float8_e4m3fn, 7), "e5m2": (ml_dtypes.float8_e5m2, 14)}[fmt]
    v = np.moveaxis(np.asarray(x, np.float32).astype(ml_dtypes.bfloat16).astype(np.float64), axis, -1)
    blocks = v.reshape(v.shape[:-1] + (-1, 32))
    amax = np.abs(blocks).max(-1, keepdims=True)
    byte = np.maximum(np.where(amax > 0, np.frexp(amax)[1] - 1 + 127, 0) - down, 1)
    scale = np.exp2(byte - 127.0)
    codes = (blocks / scale).astype(np.float32).astype(dtype).astype(np.float64)
    return np.moveaxis((codes * scale).reshape(v.shape), -1, axis)


WIDE = False


def mx_kscale(k):
    if not WIDE:
        return np.ones(k)
    levels = np.array([10, -10, 5, -5, 0])
    if k % 512:
        return np.exp2(np.random.permutation(np.resize(levels, k // 32))).repeat(32)
    a = np.empty((k // 512, 16))
    for p in range(k // 512):
        a[p, :8] = np.random.permutation(np.resize(levels, 8))
        for g in range(8):
            far = levels[np.abs(levels - a[p, g]) >= 10]
            a[p, g + 8] = far[np.random.randint(len(far))]
    return np.exp2(a.ravel()).repeat(32)


def f64(x):
    return np.asarray(x).astype(np.float64)


def striped(idx):
    return np.tile(np.asarray(idx).reshape(-1, 16).T, (8, 1)).astype(np.uint16)


def unstriped(offs):
    return offs[:16].T.reshape(-1).astype(np.int64)


B, N, T, D, DV, NQ = 4, 512, 4096, 512, 512, 128


def setup_inputs():
    n = np.random.standard_normal
    seg = T // B
    idx = np.concatenate([b * seg + np.random.permutation(seg)[:N] for b in range(B)])
    s = mx_kscale(D)[:, None]
    u = np.ones(T)
    u[idx] = mx_kscale(B * N)
    r = np.random.uniform(0.5, 2.0, T)
    raw = n((D, T)) / s / (u * r)
    return {
        "qT": (n((B, D, NQ)) * s * (1.00 / np.sqrt(D))).astype(np.float32),
        "cT": raw.astype(np.float32),
        "ts": np.tile(u * r, (128, 1)).astype(np.float32),
        "kb": np.tile(n(T), (128, 1)).astype(np.float32),
        "ch": np.tile(s[:, 0] * np.random.uniform(0.5, 2.0, D), (128, 1)).astype(np.float32),
        "offs": striped(idx),
    }


def reference(qT, cT, ts, kb, ch, offs):
    idx = unstriped(offs)
    c = f64(cT)
    pick = lambda x: x[:, idx].reshape(x.shape[0], B, N).transpose(1, 0, 2)
    q = f64(qT)
    score = mxq(q, 1, "e4m3").transpose(0, 2, 1) @ mxq(pick(c), 1, "e4m3")
    score = score * pick(f64(ts))[:, :1, :]
    score = score + pick(f64(kb))[:, :1, :]
    p = 1.0 / (1.0 + np.exp(-score))
    w = p * pick(f64(ts))[:, :1, :]
    y = mxq(w, 2, "e4m3") @ mxq(pick(c).transpose(0, 2, 1), 1, "e4m3")
    y = y / 16.0
    y = y * f64(ch)[:1]
    return y

@@ -1,0 +1,167 @@
+from contextlib import ExitStack
+
+import concourse.mybir as mybir
+from concourse.masks import make_identity
+
+B, N, T, D, NQ = 4, 512, 4096, 512, 128
+P = 128
+SEG = T // B
+
+FLOPS = B * 2 * (2 * N * D * NQ)
+BYTES = 4 * (B * D * NQ + D * T + 2 * T + D + B * NQ * D) + 2 * P * (B * N // 16)
+
+F32 = mybir.dt.float32
+BF16 = mybir.dt.bfloat16
+U32 = mybir.dt.uint32
+U16 = mybir.dt.uint16
+U8 = mybir.dt.uint8
+FP8X4 = mybir.dt.float8_e4m3fn_x4
+ADD, MULT = mybir.AluOpType.add, mybir.AluOpType.mult
+COPY = mybir.ActivationFunctionType.Copy
+SIGMOID = mybir.ActivationFunctionType.Sigmoid
+
+
+def tile_attend_x_mla_sigmoid_seg_kernel(tc, qT, cT, ts, kb, ch, offs, out):
+    nc = tc.nc
+    with ExitStack() as ctx:
+        keep = ctx.enter_context(tc.tile_pool(name="keep", bufs=1))
+        ring = ctx.enter_context(tc.tile_pool(name="ring", bufs=3))
+        ring2 = ctx.enter_context(tc.tile_pool(name="ring2", bufs=2))
+        psum = ctx.enter_context(tc.psum_pool(name="psum", bufs=2))
+
+        lists = keep.tile([P, B * N // 16], U16, name="lists")
+        nc.sync.dma_start(lists[:], offs)
+
+        windows = {}
+        for name, src in (("ts", ts), ("kb", kb)):
+            windows[name] = keep.tile([P, T], F32, name="win_" + name)
+        for a, b, name, src, eng in (
+            (0, SEG, "kb", kb, nc.vector),
+            (0, SEG, "ts", ts, nc.vector),
+            (SEG, T, "kb", kb, nc.vector),
+            (SEG, T, "ts", ts, nc.gpsimd),
+        ):
+            eng.memset(windows[name][:, a:b], 0.0)
+            nc.scalar.dma_start(windows[name][0:1, a:b], src[0:1, a:b])
+
+        warm = keep.tile([P, 1], F32, name="warm")
+        nc.vector.memset(warm[:], 0.0)
+        warm_out = keep.tile([P, 1], F32, name="warm_out")
+        nc.scalar.activation(warm_out[:], warm[:], SIGMOID)
+
+        ident = keep.tile([P, P], F32, name="ident")
+        make_identity(nc, ident[:])
+
+        cT_v = cT.rearrange("(p j) w -> p j w", j=4)
+        raw = {}
+        q_raw = keep.tile([P, B, 4, NQ], F32, name="q_raw")
+        chans = keep.tile([P, D], F32, name="chans")
+        for b in range(B):
+            for u in range(2):
+                r = keep.tile([P, 2, SEG], F32, name=f"raw{b}{u}")
+                nc.sync.dma_start(r[:], cT_v[:, 2 * u : 2 * u + 2, b * SEG : (b + 1) * SEG])
+                raw[b, u] = r
+            if b == 0:
+                nc.sync.dma_start(
+                    q_raw[:].rearrange("p b j q -> p b (j q)"),
+                    qT.rearrange("b (p j) q -> p b (j q)", j=4),
+                )
+        nc.sync.dma_start(chans[:], ch)
+
+        cols = {}
+
+        q_grp = keep.tile([P, B * NQ * 4], BF16, align_bytes=64, name="q_grp")
+        for b in range(B):
+            nc.gpsimd.tensor_scalar(
+                out=q_grp[:, b * NQ * 4 : (b + 1) * NQ * 4].rearrange("p (q j) -> p q j", j=4),
+                in0=q_raw[:, b].rearrange("p j q -> p q j"),
+                scalar1=1.0, scalar2=0.0, op0=MULT, op1=ADD,
+            )
+        q_codes = keep.tile([P, B * NQ], U32, align_bytes=64, name="q_codes")
+        q_scales = keep.tile([P, B * NQ], U8, align_bytes=64, name="q_scales")
+
+        pool = [keep.tile([P, 2 * T], BF16, name=f"pool{u}") for u in range(2)]
+
+        for b in range(B):
+            for name in ("kb", "ts"):
+                g = ring.tile([P, N], F32, name="got_" + name)
+                win = windows[name][:, 0 : (b + 1) * SEG]
+                nc.vector.tensor_copy(g[:], win.indirect(lists[:, b * 32 : (b + 1) * 32]))
+                pt = psum.tile([P, 4, P], F32, name="pt")
+                view = g[:].rearrange("p (s t) -> p t s", t=4)
+                for t in range(4):
+                    nc.tensor.transpose(pt[:, t, :], view[:, t, :], ident[:])
+                c = keep.tile([P, 4], F32, name=f"col_{name}{b}")
+                nc.scalar.copy(c[:], pt[:, :, 0])
+                cols[name, b] = c
+            k_grp = ring.tile([P, N * 4], BF16, align_bytes=64, name="k_grp")
+            k_out = k_grp[:].bitcast(U32).rearrange("p (t s u) -> p s t u", t=4, u=2)
+            k_words = k_grp[:].bitcast(F32).rearrange("p (t s u) -> p t s u", t=4, u=2)
+            v_grp = ring.tile([P, D * 4], BF16, align_bytes=64, name="v_grp")
+            for u in range(2):
+                nc.scalar.activation(
+                    pool[u][:, 2 * b * SEG : 2 * (b + 1) * SEG].rearrange("p (w e) -> p w e", e=2),
+                    raw[b, u][:].rearrange("p e w -> p w e"),
+                    COPY,
+                )
+            for u in range(2):
+                win = pool[u][:].bitcast(U32)[:, 0 : (b + 1) * SEG]
+                nc.vector.tensor_copy(k_out[:, :, :, u], win.indirect(lists[:, b * 32 : (b + 1) * 32]))
+            k_codes = ring.tile([P, N], U32, align_bytes=64, name="k_codes")
+            k_scales = ring.tile([P, N], U8, align_bytes=64, name="k_scales")
+            if b == 0:
+                nc.vector.quantize_mx(out=q_codes[:].bitcast(FP8X4), scales=q_scales[:], in_=q_grp[:])
+            nc.vector.quantize_mx(out=k_codes[:].bitcast(FP8X4), scales=k_scales[:], in_=k_grp[:])
+            scores = psum.tile([P, 4, NQ], F32, name="scores")
+            for t in range(4):
+                nc.tensor.matmul_mx(
+                    out=scores[:, t, :],
+                    lhsT=k_codes[:, t * P : (t + 1) * P].bitcast(FP8X4),
+                    lhsT_scale=k_scales[:, t * P : (t + 1) * P],
+                    rhs=q_codes[:, b * NQ : (b + 1) * NQ].bitcast(FP8X4),
+                    rhs_scale=q_scales[:, b * NQ : (b + 1) * NQ],
+                    start=True, stop=True,
+                )
+            p = ring2.tile([P, 4, NQ], F32, name="p")
+            for t in range(4):
+                nc.scalar.activation(
+                    p[:, t, :], scores[:, t, :], SIGMOID,
+                    bias=cols["kb", b][:, t : t + 1], scale=cols["ts", b][:, t : t + 1],
+                )
+            for u in range(2):
+                pv = psum.tile([P, 4, P], F32, name="pv")
+                for t in range(4):
+                    nc.tensor.transpose(pv[:, t, :], k_words[:, t, :, u], ident[:])
+                nc.scalar.copy(
+                    v_grp[:, u * 1024 : (u + 1) * 1024].rearrange("s (e m t) -> s e m t", e=2, t=4),
+                    pv[:].bitcast(BF16).rearrange("s t (m e) -> s e m t", e=2),
+                )
+            w_grp = ring2.tile([P, NQ, 4], BF16, align_bytes=64, name="w_grp")
+            nc.vector.tensor_tensor(
+                w_grp[:], p[:].rearrange("s t q -> s q t"),
+                cols["ts", b][:].unsqueeze(1).to_broadcast([P, NQ, 4]), MULT,
+            )
+            v_codes = ring.tile([P, D], U32, align_bytes=64, name="v_codes")
+            v_scales = ring.tile([P, D], U8, align_bytes=64, name="v_scales")
+            nc.vector.quantize_mx(out=v_codes[:].bitcast(FP8X4), scales=v_scales[:], in_=v_grp[:])
+            w_codes = ring2.tile([P, NQ], U32, align_bytes=64, name="w_codes")
+            w_scales = ring2.tile([P, NQ], U8, align_bytes=64, name="w_scales")
+            nc.vector.quantize_mx(
+                out=w_codes[:].bitcast(FP8X4), scales=w_scales[:], in_=w_grp[:].rearrange("s q t -> s (q t)")
+            )
+            acc = psum.tile([P, D], F32, name="acc")
+            nc.tensor.matmul_mx(
+                out=acc[:],
+                lhsT=w_codes[:].bitcast(FP8X4), lhsT_scale=w_scales[:],
+                rhs=v_codes[:].bitcast(FP8X4), rhs_scale=v_scales[:],
+                start=True, stop=True,
+            )
+            y = ring2.tile([P, D], F32, name="y")
+            nc.vector.scalar_tensor_tensor(
+                out=y[:].rearrange("q (p j) -> q p j", j=4),
+                in0=acc[:].rearrange("q (j p) -> q p j", j=4),
+                scalar=1.0 / 16.0,
+                in1=chans[:].rearrange("q (p j) -> q p j", j=4),
+                op0=MULT, op1=MULT,
+            )
+            nc.sync.dma_start(out[b], y[:])

@@ -6,9 +6,13 @@ from concourse.masks import make_identity
 B, N, T, D, NQ = 4, 512, 4096, 512, 128
 P = 128
 SEG = T // B
+LANES = 4
+LIST_COLUMNS = N // 16
 
 FLOPS = B * 2 * (2 * N * D * NQ)
 BYTES = 4 * (B * D * NQ + D * T + 2 * T + D + B * NQ * D) + 2 * P * (B * N // 16)
+
+CAST_ON_VECTOR = ((1, 1), (3, 1))
 
 F32 = mybir.dt.float32
 BF16 = mybir.dt.bfloat16
@@ -16,7 +20,7 @@ U32 = mybir.dt.uint32
 U16 = mybir.dt.uint16
 U8 = mybir.dt.uint8
 FP8X4 = mybir.dt.float8_e4m3fn_x4
-ADD, MULT = mybir.AluOpType.add, mybir.AluOpType.mult
+MULT = mybir.AluOpType.mult
 COPY = mybir.ActivationFunctionType.Copy
 SIGMOID = mybir.ActivationFunctionType.Sigmoid
 
@@ -25,143 +29,236 @@ def tile_attend_x_mla_sigmoid_seg_kernel(tc, qT, cT, ts, kb, ch, offs, out):
     nc = tc.nc
     with ExitStack() as ctx:
         keep = ctx.enter_context(tc.tile_pool(name="keep", bufs=1))
-        ring = ctx.enter_context(tc.tile_pool(name="ring", bufs=3))
+        ring3 = ctx.enter_context(tc.tile_pool(name="ring3", bufs=3))
         ring2 = ctx.enter_context(tc.tile_pool(name="ring2", bufs=2))
-        psum = ctx.enter_context(tc.psum_pool(name="psum", bufs=2))
+        psum2 = ctx.enter_context(tc.psum_pool(name="psum2", bufs=2))
+        psum4 = ctx.enter_context(tc.psum_pool(name="psum4", bufs=4))
 
         lists = keep.tile([P, B * N // 16], U16, name="lists")
         nc.sync.dma_start(lists[:], offs)
-
-        windows = {}
-        for name, src in (("ts", ts), ("kb", kb)):
-            windows[name] = keep.tile([P, T], F32, name="win_" + name)
-        for a, b, name, src, eng in (
-            (0, SEG, "kb", kb, nc.vector),
-            (0, SEG, "ts", ts, nc.vector),
-            (SEG, T, "kb", kb, nc.vector),
-            (SEG, T, "ts", ts, nc.gpsimd),
-        ):
-            eng.memset(windows[name][:, a:b], 0.0)
-            nc.scalar.dma_start(windows[name][0:1, a:b], src[0:1, a:b])
 
         warm = keep.tile([P, 1], F32, name="warm")
         nc.vector.memset(warm[:], 0.0)
         warm_out = keep.tile([P, 1], F32, name="warm_out")
         nc.scalar.activation(warm_out[:], warm[:], SIGMOID)
 
+        windows = {}
+        for name in ("ts", "kb"):
+            windows[name] = keep.tile([P, T], F32, name="window_" + name)
+        raw_first = keep.tile([P, 2, 2, SEG], F32, name="raw_first")
+        raw_later = keep.tile([P, 2 * (B - 1), 2, SEG], F32, name="raw_later")
+        q_raw = keep.tile([P, B, LANES, NQ], F32, name="q_raw")
+        chans = keep.tile([P, D], F32, name="chans")
+
+        def raw(b, u):
+            return raw_first[:, u] if b == 0 else raw_later[:, 2 * (b - 1) + u]
+
+        nc.vector.memset(windows["kb"][:, 0:SEG], 0.0)
+        nc.gpsimd.memset(windows["ts"][:, 0:SEG], 0.0)
+        nc.vector.memset(windows["kb"][:, SEG:T], 0.0)
+        nc.gpsimd.memset(windows["ts"][:, SEG:T], 0.0)
         ident = keep.tile([P, P], F32, name="ident")
         make_identity(nc, ident[:])
 
-        cT_v = cT.rearrange("(p j) w -> p j w", j=4)
-        raw = {}
-        q_raw = keep.tile([P, B, 4, NQ], F32, name="q_raw")
-        chans = keep.tile([P, D], F32, name="chans")
-        for b in range(B):
-            for u in range(2):
-                r = keep.tile([P, 2, SEG], F32, name=f"raw{b}{u}")
-                nc.sync.dma_start(r[:], cT_v[:, 2 * u : 2 * u + 2, b * SEG : (b + 1) * SEG])
-                raw[b, u] = r
-            if b == 0:
+        def load_rows(c0, c1):
+            for name, src in (("kb", kb), ("ts", ts)):
+                nc.sync.dma_start(windows[name][0:1, c0:c1], src[0:1, c0:c1])
+
+        cT_view = cT.rearrange("(p j) w -> p j w", j=LANES)
+
+        def load_pool(b, u, pieces=1):
+            w = SEG // pieces
+            for i in range(pieces):
                 nc.sync.dma_start(
-                    q_raw[:].rearrange("p b j q -> p b (j q)"),
-                    qT.rearrange("b (p j) q -> p b (j q)", j=4),
+                    raw(b, u)[:, :, i * w : (i + 1) * w],
+                    cT_view[:, 2 * u : 2 * u + 2, b * SEG + i * w : b * SEG + (i + 1) * w],
                 )
+
+        load_rows(0, SEG)
+        load_pool(0, 0, pieces=2)
+        load_pool(0, 1)
+        load_rows(SEG, T)
+        load_pool(1, 0)
+        nc.sync.dma_start(
+            q_raw[:].rearrange("p b j q -> p b (j q)"),
+            qT.rearrange("b (p j) q -> p b (j q)", j=LANES),
+        )
+        load_pool(1, 1)
+        for b in range(2, B):
+            load_pool(b, 0)
+            load_pool(b, 1)
         nc.sync.dma_start(chans[:], ch)
 
-        cols = {}
-
-        q_grp = keep.tile([P, B * NQ * 4], BF16, align_bytes=64, name="q_grp")
-        for b in range(B):
-            nc.gpsimd.tensor_scalar(
-                out=q_grp[:, b * NQ * 4 : (b + 1) * NQ * 4].rearrange("p (q j) -> p q j", j=4),
-                in0=q_raw[:, b].rearrange("p j q -> p q j"),
-                scalar1=1.0, scalar2=0.0, op0=MULT, op1=ADD,
-            )
+        q_grp = keep.tile([P, B * NQ * LANES], BF16, align_bytes=64, name="q_grp")
         q_codes = keep.tile([P, B * NQ], U32, align_bytes=64, name="q_codes")
         q_scales = keep.tile([P, B * NQ], U8, align_bytes=64, name="q_scales")
 
         pool = [keep.tile([P, 2 * T], BF16, name=f"pool{u}") for u in range(2)]
+        k_grp, tokens, scores, turned, acc = {}, {}, {}, {}, {}
+        v_codes, v_scales = {}, {}
+        token_rows = {}
 
-        for b in range(B):
+        def gather_tokens(b0, b1):
             for name in ("kb", "ts"):
-                g = ring.tile([P, N], F32, name="got_" + name)
-                win = windows[name][:, 0 : (b + 1) * SEG]
-                nc.vector.tensor_copy(g[:], win.indirect(lists[:, b * 32 : (b + 1) * 32]))
-                pt = psum.tile([P, 4, P], F32, name="pt")
-                view = g[:].rearrange("p (s t) -> p t s", t=4)
-                for t in range(4):
-                    nc.tensor.transpose(pt[:, t, :], view[:, t, :], ident[:])
-                c = keep.tile([P, 4], F32, name=f"col_{name}{b}")
-                nc.scalar.copy(c[:], pt[:, :, 0])
-                cols[name, b] = c
-            k_grp = ring.tile([P, N * 4], BF16, align_bytes=64, name="k_grp")
-            k_out = k_grp[:].bitcast(U32).rearrange("p (t s u) -> p s t u", t=4, u=2)
-            k_words = k_grp[:].bitcast(F32).rearrange("p (t s u) -> p t s u", t=4, u=2)
-            v_grp = ring.tile([P, D * 4], BF16, align_bytes=64, name="v_grp")
-            for u in range(2):
-                nc.scalar.activation(
-                    pool[u][:, 2 * b * SEG : 2 * (b + 1) * SEG].rearrange("p (w e) -> p w e", e=2),
-                    raw[b, u][:].rearrange("p e w -> p w e"),
-                    COPY,
-                )
-            for u in range(2):
-                win = pool[u][:].bitcast(U32)[:, 0 : (b + 1) * SEG]
-                nc.vector.tensor_copy(k_out[:, :, :, u], win.indirect(lists[:, b * 32 : (b + 1) * 32]))
-            k_codes = ring.tile([P, N], U32, align_bytes=64, name="k_codes")
-            k_scales = ring.tile([P, N], U8, align_bytes=64, name="k_scales")
+                row = keep.tile([P, (b1 - b0) * N], F32, name=f"row_{name}{b0}")
+                window = windows[name][:, 0 : b1 * SEG]
+                nc.vector.tensor_copy(row[:], window.indirect(lists[:, b0 * LIST_COLUMNS : b1 * LIST_COLUMNS]))
+                token_rows[name, b0] = row
+
+        def turn_tokens(b0, b1, bank):
+            n = b1 - b0
+            for i, name in enumerate(("kb", "ts")):
+                view = token_rows[name, b0][:].rearrange("p (b s t) -> p b t s", t=LANES, b=n)
+                for b in range(n):
+                    for t in range(LANES):
+                        c0 = 2 * ((i * n + b) * LANES + t)
+                        nc.tensor.transpose(bank[:, c0 : c0 + P], view[:, b, t, :], ident[:])
+            columns = keep.tile([P, 2, n, LANES], F32, name=f"columns{b0}")
+            nc.vector.tensor_copy(
+                columns[:].rearrange("s i b t -> s (i b t)"),
+                bank[:, 0 : 4 * LANES * n].rearrange("s (i z) -> s i z", z=2)[:, :, 0],
+            )
+            for b in range(n):
+                tokens[b0 + b] = columns[:, :, b, :]
+
+        def cast(b, u, pieces=1):
+            w = SEG // pieces
+            for i in range(pieces):
+                c0 = 2 * (b * SEG + i * w)
+                pair_out = pool[u][:, c0 : c0 + 2 * w].rearrange("p (w e) -> p w e", e=2)
+                pair_in = raw(b, u)[:, :, i * w : (i + 1) * w].rearrange("p e w -> p w e")
+                if (b, u) in CAST_ON_VECTOR:
+                    nc.vector.tensor_copy(pair_out, pair_in)
+                else:
+                    nc.scalar.activation(pair_out, pair_in, COPY)
+
+        def gather(b, u):
+            if u == 0:
+                k_grp[b] = ring3.tile([P, N * LANES], BF16, align_bytes=64, name="k_grp")
+            words = k_grp[b][:].bitcast(U32).rearrange("p (t s u) -> p s t u", t=LANES, u=2)
+            window = pool[u][:].bitcast(U32)[:, 0 : (b + 1) * SEG]
+            nc.vector.tensor_copy(
+                words[:, :, :, u], window.indirect(lists[:, b * LIST_COLUMNS : (b + 1) * LIST_COLUMNS])
+            )
+
+        def turn(b, u):
+            words = k_grp[b][:].bitcast(F32).rearrange("p (t s u) -> p t s u", t=LANES, u=2)
+            turned[b, u] = psum4.tile([P, LANES, P], F32, tag="turned", name=f"turned{b}{u}")
+            for t in range(LANES):
+                nc.tensor.transpose(turned[b, u][:, t, :], words[:, t, :, u], ident[:])
+
+        def cast_queries():
+            nc.scalar.activation(
+                q_grp[:].rearrange("p (b q j) -> p b q j", b=B, j=LANES), q_raw[:].rearrange("p b j q -> p b q j"), COPY
+            )
+
+        def score(b):
+            cols = slice(b * NQ, (b + 1) * NQ)
             if b == 0:
                 nc.vector.quantize_mx(out=q_codes[:].bitcast(FP8X4), scales=q_scales[:], in_=q_grp[:])
-            nc.vector.quantize_mx(out=k_codes[:].bitcast(FP8X4), scales=k_scales[:], in_=k_grp[:])
-            scores = psum.tile([P, 4, NQ], F32, name="scores")
-            for t in range(4):
+            k_codes = ring3.tile([P, N], U32, align_bytes=64, name="k_codes")
+            k_scales = ring3.tile([P, N], U8, align_bytes=64, name="k_scales")
+            nc.vector.quantize_mx(out=k_codes[:].bitcast(FP8X4), scales=k_scales[:], in_=k_grp[b][:])
+            scores[b] = psum2.tile([P, LANES, NQ], F32, name="scores")
+            for t in range(LANES):
                 nc.tensor.matmul_mx(
-                    out=scores[:, t, :],
+                    out=scores[b][:, t, :],
                     lhsT=k_codes[:, t * P : (t + 1) * P].bitcast(FP8X4),
                     lhsT_scale=k_scales[:, t * P : (t + 1) * P],
-                    rhs=q_codes[:, b * NQ : (b + 1) * NQ].bitcast(FP8X4),
-                    rhs_scale=q_scales[:, b * NQ : (b + 1) * NQ],
-                    start=True, stop=True,
+                    rhs=q_codes[:, cols].bitcast(FP8X4),
+                    rhs_scale=q_scales[:, cols],
+                    start=True,
+                    stop=True,
                 )
-            p = ring2.tile([P, 4, NQ], F32, name="p")
-            for t in range(4):
-                nc.scalar.activation(
-                    p[:, t, :], scores[:, t, :], SIGMOID,
-                    bias=cols["kb", b][:, t : t + 1], scale=cols["ts", b][:, t : t + 1],
-                )
+
+        def values(b):
+            v_grp = ring3.tile([P, D * LANES], BF16, align_bytes=64, name="v_grp")
+            half = D * LANES // 2
             for u in range(2):
-                pv = psum.tile([P, 4, P], F32, name="pv")
-                for t in range(4):
-                    nc.tensor.transpose(pv[:, t, :], k_words[:, t, :, u], ident[:])
                 nc.scalar.copy(
-                    v_grp[:, u * 1024 : (u + 1) * 1024].rearrange("s (e m t) -> s e m t", e=2, t=4),
-                    pv[:].bitcast(BF16).rearrange("s t (m e) -> s e m t", e=2),
+                    v_grp[:, u * half : (u + 1) * half].rearrange("s (e m t) -> s e m t", e=2, t=LANES),
+                    turned[b, u][:].bitcast(BF16).rearrange("s t (m e) -> s e m t", e=2),
                 )
-            w_grp = ring2.tile([P, NQ, 4], BF16, align_bytes=64, name="w_grp")
+            v_codes[b] = ring3.tile([P, D], U32, align_bytes=64, name="v_codes")
+            v_scales[b] = ring3.tile([P, D], U8, align_bytes=64, name="v_scales")
+            nc.vector.quantize_mx(out=v_codes[b][:].bitcast(FP8X4), scales=v_scales[b][:], in_=v_grp[:])
+
+        def weights(b):
+            bias, scale = tokens[b][:, 0, :], tokens[b][:, 1, :]
+            p = ring2.tile([P, LANES, NQ], F32, name="p")
+            for t in range(LANES):
+                nc.scalar.activation(
+                    p[:, t, :],
+                    scores[b][:, t, :],
+                    SIGMOID,
+                    bias=bias[:, t : t + 1],
+                    scale=scale[:, t : t + 1],
+                )
+            w_grp = ring2.tile([P, NQ, LANES], BF16, align_bytes=64, name="w_grp")
             nc.vector.tensor_tensor(
-                w_grp[:], p[:].rearrange("s t q -> s q t"),
-                cols["ts", b][:].unsqueeze(1).to_broadcast([P, NQ, 4]), MULT,
+                w_grp[:],
+                p[:].rearrange("s t q -> s q t"),
+                scale.unsqueeze(1).to_broadcast([P, NQ, LANES]),
+                MULT,
             )
-            v_codes = ring.tile([P, D], U32, align_bytes=64, name="v_codes")
-            v_scales = ring.tile([P, D], U8, align_bytes=64, name="v_scales")
-            nc.vector.quantize_mx(out=v_codes[:].bitcast(FP8X4), scales=v_scales[:], in_=v_grp[:])
             w_codes = ring2.tile([P, NQ], U32, align_bytes=64, name="w_codes")
             w_scales = ring2.tile([P, NQ], U8, align_bytes=64, name="w_scales")
             nc.vector.quantize_mx(
                 out=w_codes[:].bitcast(FP8X4), scales=w_scales[:], in_=w_grp[:].rearrange("s q t -> s (q t)")
             )
-            acc = psum.tile([P, D], F32, name="acc")
+            acc[b] = psum2.tile([P, D], F32, tag="acc", name=f"acc{b}")
             nc.tensor.matmul_mx(
-                out=acc[:],
-                lhsT=w_codes[:].bitcast(FP8X4), lhsT_scale=w_scales[:],
-                rhs=v_codes[:].bitcast(FP8X4), rhs_scale=v_scales[:],
-                start=True, stop=True,
+                out=acc[b][:],
+                lhsT=w_codes[:].bitcast(FP8X4),
+                lhsT_scale=w_scales[:],
+                rhs=v_codes[b][:].bitcast(FP8X4),
+                rhs_scale=v_scales[b][:],
+                start=True,
+                stop=True,
             )
+
+        def finish(b):
             y = ring2.tile([P, D], F32, name="y")
             nc.vector.scalar_tensor_tensor(
-                out=y[:].rearrange("q (p j) -> q p j", j=4),
-                in0=acc[:].rearrange("q (j p) -> q p j", j=4),
+                out=y[:].rearrange("q (m j) -> q m j", j=LANES),
+                in0=acc[b][:].rearrange("q (j m) -> q m j", j=LANES),
                 scalar=1.0 / 16.0,
-                in1=chans[:].rearrange("q (p j) -> q p j", j=4),
-                op0=MULT, op1=MULT,
+                in1=chans[:].rearrange("q (m j) -> q m j", j=LANES),
+                op0=MULT,
+                op1=MULT,
             )
             nc.sync.dma_start(out[b], y[:])
+
+        gather_tokens(0, 1)
+        bank0 = psum2.tile([P, 512], F32, tag="acc", name="bank0")
+        turn_tokens(0, 1, bank0)
+        cast(0, 0, pieces=2)
+        cast(0, 1)
+        gather(0, 0)
+        turn(0, 0)
+        gather(0, 1)
+        turn(0, 1)
+        gather_tokens(1, B)
+        cast_queries()
+        score(0)
+        for b in range(1, B):
+            cast(b, 0)
+            cast(b, 1)
+            gather(b, 0)
+            gather(b, 1)
+            if b >= 2:
+                weights(b - 2)
+            values(b - 1)
+            turn(b, 0)
+            turn(b, 1)
+            if b == 1:
+                bank1 = psum4.tile([P, 512], F32, tag="turned", name="bank1")
+                turn_tokens(1, B, bank1)
+            score(b)
+            if b >= 2:
+                finish(b - 2)
+        weights(B - 2)
+        values(B - 1)
+        finish(B - 2)
+        weights(B - 1)
+        finish(B - 1)

from contextlib import ExitStack

import concourse.mybir as mybir
from concourse.masks import make_identity

B, N, T, D, NQ = 4, 512, 4096, 512, 128
P = 128
SEG = T // B
LANES = 4
LIST_COLUMNS = N // 16

FLOPS = B * 2 * (2 * N * D * NQ)
BYTES = 4 * (B * D * NQ + D * T + 2 * T + D + B * NQ * D) + 2 * P * (B * N // 16)

CAST_ON_VECTOR = ((1, 1), (3, 1))

F32 = mybir.dt.float32
BF16 = mybir.dt.bfloat16
U32 = mybir.dt.uint32
U16 = mybir.dt.uint16
U8 = mybir.dt.uint8
FP8X4 = mybir.dt.float8_e4m3fn_x4
MULT = mybir.AluOpType.mult
COPY = mybir.ActivationFunctionType.Copy
SIGMOID = mybir.ActivationFunctionType.Sigmoid


def tile_attend_x_mla_sigmoid_seg_kernel(tc, qT, cT, ts, kb, ch, offs, out):
    nc = tc.nc
    with ExitStack() as ctx:
        keep = ctx.enter_context(tc.tile_pool(name="keep", bufs=1))
        ring3 = ctx.enter_context(tc.tile_pool(name="ring3", bufs=3))
        ring2 = ctx.enter_context(tc.tile_pool(name="ring2", bufs=2))
        psum2 = ctx.enter_context(tc.psum_pool(name="psum2", bufs=2))
        psum4 = ctx.enter_context(tc.psum_pool(name="psum4", bufs=4))

        lists = keep.tile([P, B * N // 16], U16, name="lists")
        nc.sync.dma_start(lists[:], offs)

        warm = keep.tile([P, 1], F32, name="warm")
        nc.vector.memset(warm[:], 0.0)
        warm_out = keep.tile([P, 1], F32, name="warm_out")
        nc.scalar.activation(warm_out[:], warm[:], SIGMOID)

        windows = {}
        for name in ("ts", "kb"):
            windows[name] = keep.tile([P, T], F32, name="window_" + name)
        raw_first = keep.tile([P, 2, 2, SEG], F32, name="raw_first")
        raw_later = keep.tile([P, 2 * (B - 1), 2, SEG], F32, name="raw_later")
        q_raw = keep.tile([P, B, LANES, NQ], F32, name="q_raw")
        chans = keep.tile([P, D], F32, name="chans")

        def raw(b, u):
            return raw_first[:, u] if b == 0 else raw_later[:, 2 * (b - 1) + u]

        nc.vector.memset(windows["kb"][:, 0:SEG], 0.0)
        nc.gpsimd.memset(windows["ts"][:, 0:SEG], 0.0)
        nc.vector.memset(windows["kb"][:, SEG:T], 0.0)
        nc.gpsimd.memset(windows["ts"][:, SEG:T], 0.0)
        ident = keep.tile([P, P], F32, name="ident")
        make_identity(nc, ident[:])

        def load_rows(c0, c1):
            for name, src in (("kb", kb), ("ts", ts)):
                nc.sync.dma_start(windows[name][0:1, c0:c1], src[0:1, c0:c1])

        cT_view = cT.rearrange("(p j) w -> p j w", j=LANES)

        def load_pool(b, u, pieces=1):
            w = SEG // pieces
            for i in range(pieces):
                nc.sync.dma_start(
                    raw(b, u)[:, :, i * w : (i + 1) * w],
                    cT_view[:, 2 * u : 2 * u + 2, b * SEG + i * w : b * SEG + (i + 1) * w],
                )

        load_rows(0, SEG)
        load_pool(0, 0, pieces=2)
        load_pool(0, 1)
        load_rows(SEG, T)
        load_pool(1, 0)
        nc.sync.dma_start(
            q_raw[:].rearrange("p b j q -> p b (j q)"),
            qT.rearrange("b (p j) q -> p b (j q)", j=LANES),
        )
        load_pool(1, 1)
        for b in range(2, B):
            load_pool(b, 0)
            load_pool(b, 1)
        nc.sync.dma_start(chans[:], ch)

        q_grp = keep.tile([P, B * NQ * LANES], BF16, align_bytes=64, name="q_grp")
        q_codes = keep.tile([P, B * NQ], U32, align_bytes=64, name="q_codes")
        q_scales = keep.tile([P, B * NQ], U8, align_bytes=64, name="q_scales")

        pool = [keep.tile([P, 2 * T], BF16, name=f"pool{u}") for u in range(2)]
        k_grp, tokens, scores, turned, acc = {}, {}, {}, {}, {}
        v_codes, v_scales = {}, {}
        token_rows = {}

        def gather_tokens(b0, b1):
            for name in ("kb", "ts"):
                row = keep.tile([P, (b1 - b0) * N], F32, name=f"row_{name}{b0}")
                window = windows[name][:, 0 : b1 * SEG]
                nc.vector.tensor_copy(row[:], window.indirect(lists[:, b0 * LIST_COLUMNS : b1 * LIST_COLUMNS]))
                token_rows[name, b0] = row

        def turn_tokens(b0, b1, bank):
            n = b1 - b0
            for i, name in enumerate(("kb", "ts")):
                view = token_rows[name, b0][:].rearrange("p (b s t) -> p b t s", t=LANES, b=n)
                for b in range(n):
                    for t in range(LANES):
                        c0 = 2 * ((i * n + b) * LANES + t)
                        nc.tensor.transpose(bank[:, c0 : c0 + P], view[:, b, t, :], ident[:])
            columns = keep.tile([P, 2, n, LANES], F32, name=f"columns{b0}")
            nc.vector.tensor_copy(
                columns[:].rearrange("s i b t -> s (i b t)"),
                bank[:, 0 : 4 * LANES * n].rearrange("s (i z) -> s i z", z=2)[:, :, 0],
            )
            for b in range(n):
                tokens[b0 + b] = columns[:, :, b, :]

        def cast(b, u, pieces=1):
            w = SEG // pieces
            for i in range(pieces):
                c0 = 2 * (b * SEG + i * w)
                pair_out = pool[u][:, c0 : c0 + 2 * w].rearrange("p (w e) -> p w e", e=2)
                pair_in = raw(b, u)[:, :, i * w : (i + 1) * w].rearrange("p e w -> p w e")
                if (b, u) in CAST_ON_VECTOR:
                    nc.vector.tensor_copy(pair_out, pair_in)
                else:
                    nc.scalar.activation(pair_out, pair_in, COPY)

        def gather(b, u):
            if u == 0:
                k_grp[b] = ring3.tile([P, N * LANES], BF16, align_bytes=64, name="k_grp")
            words = k_grp[b][:].bitcast(U32).rearrange("p (t s u) -> p s t u", t=LANES, u=2)
            window = pool[u][:].bitcast(U32)[:, 0 : (b + 1) * SEG]
            nc.vector.tensor_copy(
                words[:, :, :, u], window.indirect(lists[:, b * LIST_COLUMNS : (b + 1) * LIST_COLUMNS])
            )

        def turn(b, u):
            words = k_grp[b][:].bitcast(F32).rearrange("p (t s u) -> p t s u", t=LANES, u=2)
            turned[b, u] = psum4.tile([P, LANES, P], F32, tag="turned", name=f"turned{b}{u}")
            for t in range(LANES):
                nc.tensor.transpose(turned[b, u][:, t, :], words[:, t, :, u], ident[:])

        def cast_queries():
            nc.scalar.activation(
                q_grp[:].rearrange("p (b q j) -> p b q j", b=B, j=LANES), q_raw[:].rearrange("p b j q -> p b q j"), COPY
            )

        def score(b):
            cols = slice(b * NQ, (b + 1) * NQ)
            if b == 0:
                nc.vector.quantize_mx(out=q_codes[:].bitcast(FP8X4), scales=q_scales[:], in_=q_grp[:])
            k_codes = ring3.tile([P, N], U32, align_bytes=64, name="k_codes")
            k_scales = ring3.tile([P, N], U8, align_bytes=64, name="k_scales")
            nc.vector.quantize_mx(out=k_codes[:].bitcast(FP8X4), scales=k_scales[:], in_=k_grp[b][:])
            scores[b] = psum2.tile([P, LANES, NQ], F32, name="scores")
            for t in range(LANES):
                nc.tensor.matmul_mx(
                    out=scores[b][:, t, :],
                    lhsT=k_codes[:, t * P : (t + 1) * P].bitcast(FP8X4),
                    lhsT_scale=k_scales[:, t * P : (t + 1) * P],
                    rhs=q_codes[:, cols].bitcast(FP8X4),
                    rhs_scale=q_scales[:, cols],
                    start=True,
                    stop=True,
                )

        def values(b):
            v_grp = ring3.tile([P, D * LANES], BF16, align_bytes=64, name="v_grp")
            half = D * LANES // 2
            for u in range(2):
                nc.scalar.copy(
                    v_grp[:, u * half : (u + 1) * half].rearrange("s (e m t) -> s e m t", e=2, t=LANES),
                    turned[b, u][:].bitcast(BF16).rearrange("s t (m e) -> s e m t", e=2),
                )
            v_codes[b] = ring3.tile([P, D], U32, align_bytes=64, name="v_codes")
            v_scales[b] = ring3.tile([P, D], U8, align_bytes=64, name="v_scales")
            nc.vector.quantize_mx(out=v_codes[b][:].bitcast(FP8X4), scales=v_scales[b][:], in_=v_grp[:])

        def weights(b):
            bias, scale = tokens[b][:, 0, :], tokens[b][:, 1, :]
            p = ring2.tile([P, LANES, NQ], F32, name="p")
            for t in range(LANES):
                nc.scalar.activation(
                    p[:, t, :],
                    scores[b][:, t, :],
                    SIGMOID,
                    bias=bias[:, t : t + 1],
                    scale=scale[:, t : t + 1],
                )
            w_grp = ring2.tile([P, NQ, LANES], BF16, align_bytes=64, name="w_grp")
            nc.vector.tensor_tensor(
                w_grp[:],
                p[:].rearrange("s t q -> s q t"),
                scale.unsqueeze(1).to_broadcast([P, NQ, LANES]),
                MULT,
            )
            w_codes = ring2.tile([P, NQ], U32, align_bytes=64, name="w_codes")
            w_scales = ring2.tile([P, NQ], U8, align_bytes=64, name="w_scales")
            nc.vector.quantize_mx(
                out=w_codes[:].bitcast(FP8X4), scales=w_scales[:], in_=w_grp[:].rearrange("s q t -> s (q t)")
            )
            acc[b] = psum2.tile([P, D], F32, tag="acc", name=f"acc{b}")
            nc.tensor.matmul_mx(
                out=acc[b][:],
                lhsT=w_codes[:].bitcast(FP8X4),
                lhsT_scale=w_scales[:],
                rhs=v_codes[b][:].bitcast(FP8X4),
                rhs_scale=v_scales[b][:],
                start=True,
                stop=True,
            )

        def finish(b):
            y = ring2.tile([P, D], F32, name="y")
            nc.vector.scalar_tensor_tensor(
                out=y[:].rearrange("q (m j) -> q m j", j=LANES),
                in0=acc[b][:].rearrange("q (j m) -> q m j", j=LANES),
                scalar=1.0 / 16.0,
                in1=chans[:].rearrange("q (m j) -> q m j", j=LANES),
                op0=MULT,
                op1=MULT,
            )
            nc.sync.dma_start(out[b], y[:])

        gather_tokens(0, 1)
        bank0 = psum2.tile([P, 512], F32, tag="acc", name="bank0")
        turn_tokens(0, 1, bank0)
        cast(0, 0, pieces=2)
        cast(0, 1)
        gather(0, 0)
        turn(0, 0)
        gather(0, 1)
        turn(0, 1)
        gather_tokens(1, B)
        cast_queries()
        score(0)
        for b in range(1, B):
            cast(b, 0)
            cast(b, 1)
            gather(b, 0)
            gather(b, 1)
            if b >= 2:
                weights(b - 2)
            values(b - 1)
            turn(b, 0)
            turn(b, 1)
            if b == 1:
                bank1 = psum4.tile([P, 512], F32, tag="turned", name="bank1")
                turn_tokens(1, B, bank1)
            score(b)
            if b >= 2:
                finish(b - 2)
        weights(B - 2)
        values(B - 1)
        finish(B - 2)
        weights(B - 1)
        finish(B - 1)
